import numpy as np
import ml_dtypes

BF16 = ml_dtypes.bfloat16


def bf(x):
    return np.asarray(x, np.float32).astype(BF16)


def f32(x):
    return np.asarray(x, np.float32)


def f64(x):
    return np.asarray(x).astype(np.float64)


def striped(idx):
    return np.tile(idx.reshape(-1, 16).T, (8, 1))


S, K, M, N, D, V = 4096, 128, 512, 2048, 2, 1024


def setup_inputs():
    return {"table": bf(np.random.standard_normal((K, S))), "w": bf(np.random.standard_normal((D, K, M)) / np.sqrt(D * K)), "b": f32(0.5 * np.random.standard_normal((M, 1))), "offs": striped(np.random.permutation(np.tile(np.arange(S), 2))[:N])}


def reference(table, w, b, offs):
    idx = offs[:16].T.reshape(-1)
    x = f64(table)[:, idx]
    y = sum(f64(w)[t].T @ x[:, t * V : (t + 1) * V] for t in range(D))
    return np.tanh(y + f64(b))

@@ -1,0 +1,61 @@
+import concourse.mybir as mybir
+
+BF16, F32, U16 = mybir.dt.bfloat16, mybir.dt.float32, mybir.dt.uint16
+TANH = mybir.ActivationFunctionType.Tanh
+
+P = 128
+S = 4096
+ENDS = 2
+M = 512
+EDGES = 1024
+PIECE = 512
+HALF = PIECE // 2
+N = ENDS * EDGES
+PER_COLUMN = 16
+
+FLOPS = 2 * P * M * N
+BYTES = 2 * P * N + 2 * ENDS * P * M + 4 * M + 2 * P * (N // PER_COLUMN) + 4 * M * EDGES
+
+
+def tile_gather_matmul_kernel(tc, table, w, b, offs, out):
+    nc = tc.nc
+    with (
+        tc.tile_pool(name="held", bufs=1) as held,
+        tc.tile_pool(name="staged", bufs=(M // P) * (EDGES // HALF)) as staged,
+        tc.psum_pool(name="banks", bufs=8) as banks,
+    ):
+        offsets = held.tile([P, N // PER_COLUMN], U16, name="offsets")
+        nc.sync.dma_start(offsets[:], offs)
+        weights = held.tile([P, ENDS, M], BF16, name="weights")
+        w_by_feature = w.rearrange("t k m -> k t m")
+        nodes = held.tile([P, S], BF16, name="nodes")
+        nc.sync.dma_start(nodes[:, 0 : S // 2], table[:, 0 : S // 2])
+        nc.scalar.dma_start(nodes[:, S // 2 : S], table[:, S // 2 : S])
+        nc.scalar.dma_start(weights[:, 0, 0:P], w_by_feature[:, 0, 0:P])
+        nc.scalar.dma_start(weights[:, 1, 0:P], w_by_feature[:, 1, 0:P])
+        nc.sync.dma_start(weights[:, :, P:M], w_by_feature[:, :, P:M])
+        bias = held.tile([P, M // P], F32, name="bias")
+        nc.scalar.dma_start(bias[:], b.rearrange("(a p) o -> p (a o)", p=P))
+
+        early = held.tile([P, 1], F32, name="early")
+        nc.vector.memset(early[:], 0.0)
+        nc.scalar.activation(early[:], early[:], TANH)
+
+        for a in range(M // P):
+            for h in range(EDGES // PIECE):
+                bank = banks.tile([P, PIECE], F32, name="bank")
+                for t in range(ENDS):
+                    first = (t * EDGES + h * PIECE) // PER_COLUMN
+                    picked = nodes[:].indirect(offsets[:, first : first + PIECE // PER_COLUMN])
+                    nc.tensor.matmul(
+                        bank[:],
+                        weights[:, t, a * P : (a + 1) * P],
+                        picked,
+                        start=(t == 0),
+                        stop=(t == ENDS - 1),
+                    )
+                for c in range(0, PIECE, HALF):
+                    result = staged.tile([P, HALF], F32, name="result")
+                    nc.scalar.activation(result[:], bank[:, c : c + HALF], TANH, bias=bias[:, a : a + 1])
+                    v = h * PIECE + c
+                    nc.sync.dma_start(out[a * P : (a + 1) * P, v : v + HALF], result[:])

@@ -35,7 +35,7 @@ def tile_gather_matmul_kernel(tc, table, w, b, offs, out):
         nc.scalar.dma_start(weights[:, 1, 0:P], w_by_feature[:, 1, 0:P])
         nc.sync.dma_start(weights[:, :, P:M], w_by_feature[:, :, P:M])
         bias = held.tile([P, M // P], F32, name="bias")
-        nc.scalar.dma_start(bias[:], b.rearrange("(a p) o -> p (a o)", p=P))
+        nc.sync.dma_start(bias[:], b.rearrange("(a p) o -> p (a o)", p=P))
 
         early = held.tile([P, 1], F32, name="early")
         nc.vector.memset(early[:], 0.0)

@@ -33,7 +33,8 @@ def tile_gather_matmul_kernel(tc, table, w, b, offs, out):
         nc.scalar.dma_start(nodes[:, S // 2 : S], table[:, S // 2 : S])
         nc.scalar.dma_start(weights[:, 0, 0:P], w_by_feature[:, 0, 0:P])
         nc.scalar.dma_start(weights[:, 1, 0:P], w_by_feature[:, 1, 0:P])
-        nc.sync.dma_start(weights[:, :, P:M], w_by_feature[:, :, P:M])
+        nc.sync.dma_start(weights[:, :, P : 2 * P], w_by_feature[:, :, P : 2 * P])
+        nc.scalar.dma_start(weights[:, :, 2 * P : M], w_by_feature[:, :, 2 * P : M])
         bias = held.tile([P, M // P], F32, name="bias")
         nc.sync.dma_start(bias[:], b.rearrange("(a p) o -> p (a o)", p=P))
 

@@ -38,10 +38,6 @@ def tile_gather_matmul_kernel(tc, table, w, b, offs, out):
         bias = held.tile([P, M // P], F32, name="bias")
         nc.sync.dma_start(bias[:], b.rearrange("(a p) o -> p (a o)", p=P))
 
-        early = held.tile([P, 1], F32, name="early")
-        nc.vector.memset(early[:], 0.0)
-        nc.scalar.activation(early[:], early[:], TANH)
-
         for a in range(M // P):
             for h in range(EDGES // PIECE):
                 bank = banks.tile([P, PIECE], F32, name="bank")

@@ -12,6 +12,7 @@ PIECE = 512
 HALF = PIECE // 2
 N = ENDS * EDGES
 PER_COLUMN = 16
+ALIGN = 256
 
 FLOPS = 2 * P * M * N
 BYTES = 2 * P * N + 2 * ENDS * P * M + 4 * M + 2 * P * (N // PER_COLUMN) + 4 * M * EDGES
@@ -24,11 +25,11 @@ def tile_gather_matmul_kernel(tc, table, w, b, offs, out):
         tc.tile_pool(name="staged", bufs=(M // P) * (EDGES // HALF)) as staged,
         tc.psum_pool(name="banks", bufs=8) as banks,
     ):
-        offsets = held.tile([P, N // PER_COLUMN], U16, name="offsets")
+        offsets = held.tile([P, N // PER_COLUMN], U16, name="offsets", align_bytes=ALIGN)
         nc.sync.dma_start(offsets[:], offs)
-        weights = held.tile([P, ENDS, M], BF16, name="weights")
+        weights = held.tile([P, ENDS, M], BF16, name="weights", align_bytes=ALIGN)
         w_by_feature = w.rearrange("t k m -> k t m")
-        nodes = held.tile([P, S], BF16, name="nodes")
+        nodes = held.tile([P, S], BF16, name="nodes", align_bytes=ALIGN)
         nc.sync.dma_start(nodes[:, 0 : S // 2], table[:, 0 : S // 2])
         nc.scalar.dma_start(nodes[:, S // 2 : S], table[:, S // 2 : S])
         nc.scalar.dma_start(weights[:, 0, 0:P], w_by_feature[:, 0, 0:P])
@@ -52,7 +53,7 @@ def tile_gather_matmul_kernel(tc, table, w, b, offs, out):
                         stop=(t == ENDS - 1),
                     )
                 for c in range(0, PIECE, HALF):
-                    result = staged.tile([P, HALF], F32, name="result")
+                    result = staged.tile([P, HALF], F32, name="result", align_bytes=ALIGN)
                     nc.scalar.activation(result[:], bank[:, c : c + HALF], TANH, bias=bias[:, a : a + 1])
                     v = h * PIECE + c
                     nc.sync.dma_start(out[a * P : (a + 1) * P, v : v + HALF], result[:])

import concourse.mybir as mybir

BF16, F32, U16 = mybir.dt.bfloat16, mybir.dt.float32, mybir.dt.uint16
TANH = mybir.ActivationFunctionType.Tanh

P = 128
S = 4096
ENDS = 2
M = 512
EDGES = 1024
PIECE = 512
HALF = PIECE // 2
N = ENDS * EDGES
PER_COLUMN = 16
ALIGN = 256

FLOPS = 2 * P * M * N
BYTES = 2 * P * N + 2 * ENDS * P * M + 4 * M + 2 * P * (N // PER_COLUMN) + 4 * M * EDGES


def tile_gather_matmul_kernel(tc, table, w, b, offs, out):
    nc = tc.nc
    with (
        tc.tile_pool(name="held", bufs=1) as held,
        tc.tile_pool(name="staged", bufs=(M // P) * (EDGES // HALF)) as staged,
        tc.psum_pool(name="banks", bufs=8) as banks,
    ):
        offsets = held.tile([P, N // PER_COLUMN], U16, name="offsets", align_bytes=ALIGN)
        nc.sync.dma_start(offsets[:], offs)
        weights = held.tile([P, ENDS, M], BF16, name="weights", align_bytes=ALIGN)
        w_by_feature = w.rearrange("t k m -> k t m")
        nodes = held.tile([P, S], BF16, name="nodes", align_bytes=ALIGN)
        nc.sync.dma_start(nodes[:, 0 : S // 2], table[:, 0 : S // 2])
        nc.scalar.dma_start(nodes[:, S // 2 : S], table[:, S // 2 : S])
        nc.scalar.dma_start(weights[:, 0, 0:P], w_by_feature[:, 0, 0:P])
        nc.scalar.dma_start(weights[:, 1, 0:P], w_by_feature[:, 1, 0:P])
        nc.sync.dma_start(weights[:, :, P : 2 * P], w_by_feature[:, :, P : 2 * P])
        nc.scalar.dma_start(weights[:, :, 2 * P : M], w_by_feature[:, :, 2 * P : M])
        bias = held.tile([P, M // P], F32, name="bias")
        nc.sync.dma_start(bias[:], b.rearrange("(a p) o -> p (a o)", p=P))

        for a in range(M // P):
            for h in range(EDGES // PIECE):
                bank = banks.tile([P, PIECE], F32, name="bank")
                for t in range(ENDS):
                    first = (t * EDGES + h * PIECE) // PER_COLUMN
                    picked = nodes[:].indirect(offsets[:, first : first + PIECE // PER_COLUMN])
                    nc.tensor.matmul(
                        bank[:],
                        weights[:, t, a * P : (a + 1) * P],
                        picked,
                        start=(t == 0),
                        stop=(t == ENDS - 1),
                    )
                for c in range(0, PIECE, HALF):
                    result = staged.tile([P, HALF], F32, name="result", align_bytes=ALIGN)
                    nc.scalar.activation(result[:], bank[:, c : c + HALF], TANH, bias=bias[:, a : a + 1])
                    v = h * PIECE + c
                    nc.sync.dma_start(out[a * P : (a + 1) * P, v : v + HALF], result[:])
